import numpy as np
import ml_dtypes


def mxq(x, axis, fmt="e4m3"):
    dtype, down = {"e4m3": (ml_dtypes.float8_e4m3fn, 7), "e5m2": (ml_dtypes.float8_e5m2, 14)}[fmt]
    v = np.moveaxis(np.asarray(x, np.float32).astype(ml_dtypes.bfloat16).astype(np.float64), axis, -1)
    blocks = v.reshape(v.shape[:-1] + (-1, 32))
    amax = np.abs(blocks).max(-1, keepdims=True)
    byte = np.maximum(np.where(amax > 0, np.frexp(amax)[1] - 1 + 127, 0) - down, 1)
    scale = np.exp2(byte - 127.0)
    codes = (blocks / scale).astype(np.float32).astype(dtype).astype(np.float64)
    return np.moveaxis((codes * scale).reshape(v.shape), -1, axis)


WIDE = False


def mx_kscale(k):
    if not WIDE:
        return np.ones(k)
    levels = np.array([10, -10, 5, -5, 0])
    if k % 512:
        return np.exp2(np.random.permutation(np.resize(levels, k // 32))).repeat(32)
    a = np.empty((k // 512, 16))
    for p in range(k // 512):
        a[p, :8] = np.random.permutation(np.resize(levels, 8))
        for g in range(8):
            far = levels[np.abs(levels - a[p, g]) >= 10]
            a[p, g + 8] = far[np.random.randint(len(far))]
    return np.exp2(a.ravel()).repeat(32)


def f64(x):
    return np.asarray(x).astype(np.float64)


def striped8(idx):
    return np.asarray(idx).reshape(8, -1, 16).transpose(0, 2, 1).reshape(128, -1).astype(np.uint16)


def unstriped8(offs):
    return offs.reshape(8, 16, -1).transpose(0, 2, 1).reshape(8, -1).astype(np.int64)


def pick8(x, idx, run):
    r = np.arange(len(x))
    return x[r[:, None], idx[r % (8 * run) // run]]


E2M1 = np.array([0.0, 0.5, 1.0, 1.5, 2.0, 3.0, 4.0, 6.0, -0.0, -0.5, -1.0, -1.5, -2.0, -3.0, -4.0, -6.0])


def pack_weight(w, fmt):
    k, n = w.shape
    w = f64(np.asarray(w, np.float32).astype(ml_dtypes.bfloat16)).reshape(k // 32, 32, n)
    amax = np.abs(w).max(1)
    if fmt == "e4m3":
        byte = np.frexp(amax)[1] - 1 + 127 - 7
    else:
        mant, ex = np.frexp(amax / 6.0)
        byte = np.where(mant > 0.5, ex, ex - 1) + 127
    byte = np.clip(np.where(amax > 0, byte, 1), 1, 254)
    scaled = (w * np.exp2(127.0 - byte)[:, None, :]).reshape(k, n).astype(np.float32)
    by_word = np.ascontiguousarray(scaled.reshape(k // 512, 128, 4, n).transpose(0, 1, 3, 2))
    if fmt == "e4m3":
        words = by_word.astype(ml_dtypes.float8_e4m3fn).view(np.uint8)
    else:
        c = by_word.astype(ml_dtypes.float4_e2m1fn).view(np.uint8) & 0xF
        words = (c[..., 0::2] | (c[..., 1::2] << 4)).reshape(k // 512, 128, 2 * n)
    return np.ascontiguousarray(words), np.ascontiguousarray(byte.astype(np.uint8).reshape(k // 512, 16, n))


def unpack_weight(words, scales, fmt):
    g, _, n = scales.shape
    words = np.ascontiguousarray(words).reshape(g, 128, n, -1)
    if fmt == "e4m3":
        vals = words.view(ml_dtypes.float8_e4m3fn).astype(np.float64)
    else:
        nib = np.empty((g, 128, n, 4), np.uint8)
        nib[..., 0::2] = words & 0xF
        nib[..., 1::2] = words >> 4
        vals = E2M1[nib]
    vals = vals * np.repeat(np.exp2(scales.astype(np.float64) - 127.0), 8, axis=1)[..., None]
    return vals.transpose(0, 1, 3, 2).reshape(g * 512, n)


D, T, I, Q = 512, 1024, 512, 128


def setup_inputs():
    n = np.random.standard_normal
    idx = np.stack([np.random.permutation(T)[:I] for _ in range(8)])
    idx2 = np.stack([np.random.permutation(T)[:I] for _ in range(8)])
    idx4 = np.stack([np.random.permutation(T)[:I] for _ in range(8)])
    fd = mx_kscale(D)
    keysp = pack_weight(n((D, T)) / fd[:, None], "e2m1")
    return {
        "query": (n((D, Q)) * 0.9 / np.sqrt(D) * fd[:, None]).astype(np.float32),
        "query2": (n((D, Q)) * 0.9 / np.sqrt(D) * fd[:, None]).astype(np.float32),
        "keys_words": keysp[0],
        "keys_scales": keysp[1],
        "lam": (np.random.uniform(0.5, 1.3, (Q, 1))).astype(np.float32),
        "level": (np.random.uniform(0.05, 0.2, (Q, 1))).astype(np.float32),
        "old": (np.random.uniform(0.0, 2.0, (Q, T))).astype(np.float32),
        "gainm": (np.random.uniform(0.5, 1.5, (Q, I))).astype(np.float32),
        "offs": striped8(idx),
        "offs2": striped8(idx2),
        "offs4": striped8(idx4),
    }


def reference(query, query2, keys_words, keys_scales, lam, level, old, gainm, offs, offs2, offs4):
    idx = unstriped8(offs)
    idx2 = unstriped8(offs2)
    idx4 = unstriped8(offs4)
    keysu = unpack_weight(keys_words, keys_scales, "e2m1")
    queryq = mxq(f64(query), 0, "e4m3")
    a = queryq.T @ keysu
    query2q = mxq(f64(query2), 0, "e4m3")
    b = query2q.T @ keysu
    s = (np.maximum(pick8(a, idx, 16), pick8(b, idx2, 16)) - np.maximum(pick8(a, idx2, 16), pick8(b, idx, 16))) * f64(lam)
    p = np.exp(s - np.max(s, axis=1, keepdims=True))
    r = p / np.sum(p, axis=1, keepdims=True)
    w = np.maximum(r - np.max(r, axis=1, keepdims=True) * f64(level), 0.0)
    ws = w * f64(gainm) * 256.0
    wf = np.zeros((Q, T))
    wf[np.arange(Q)[:, None], idx4[np.arange(Q) % 128 // 16]] = ws
    y = f64(old) + wf
    return y

@@ -1,0 +1,160 @@
+from contextlib import ExitStack
+
+import concourse.mybir as mybir
+
+D, T, SLOTS, Q = 512, 1024, 512, 128
+FLOPS = 2 * 2 * D * Q * T
+
+F32 = mybir.dt.float32
+BF16 = mybir.dt.bfloat16
+I32 = mybir.dt.int32
+U32 = mybir.dt.uint32
+U16 = mybir.dt.uint16
+U8 = mybir.dt.uint8
+FP8X4 = mybir.dt.float8_e4m3fn_x4
+FP4X4 = mybir.dt.float4_e2m1fn_x4
+ALU = mybir.AluOpType
+ACT = mybir.ActivationFunctionType
+
+P = 128
+PACK = 4
+N_MM = 256
+HALF = SLOTS // 2
+LIST_COLS = SLOTS // 16
+N_OUT = 256
+FIRST = 128
+
+
+def tile_attend_exchanged_excess_moved_heads_kernel(
+    tc, query, query2, keys_words, keys_scales, lam, level, old, gainm, offs, offs2, offs4, out
+):
+    nc = tc.nc
+    with ExitStack() as ctx:
+        sb = ctx.enter_context(tc.tile_pool(name="sb", bufs=1))
+        ps = ctx.enter_context(tc.psum_pool(name="ps", bufs=1))
+
+        list1 = sb.tile([P, LIST_COLS], U16, name="list1")
+        list2 = sb.tile([P, LIST_COLS], U16, name="list2")
+        list4 = sb.tile([P, LIST_COLS], U16, name="list4")
+        raw_a = sb.tile([P, PACK, Q], F32, name="raw_a")
+        raw_b = sb.tile([P, PACK, Q], F32, name="raw_b")
+        key_codes = sb.tile([P, 2 * T], U8, name="key_codes", align_bytes=64)
+        key_scales = sb.tile([P, T], U8, name="key_scales", align_bytes=64)
+        lam_sb = sb.tile([P, 1], F32, name="lam_sb")
+        level_sb = sb.tile([P, 1], F32, name="level_sb")
+        gain_sb = sb.tile([P, SLOTS], F32, name="gain_sb")
+        old_sb = sb.tile([P, T], F32, name="old_sb")
+        placed = sb.tile([P, T], F32, name="placed")
+
+        nc.vector.memset(key_scales[:, : T // 2].bitcast(I32), 0)
+        nc.gpsimd.memset(key_scales[:, T // 2 :].bitcast(I32), 0)
+        nc.sync.dma_start(out=raw_a[:], in_=query.rearrange("(p j) q -> p j q", j=PACK))
+        nc.sync.dma_start(out=key_codes[:].bitcast(I32), in_=keys_words[0].bitcast(I32))
+        for g in range(4):
+            queue = nc.sync if g % 2 == 0 else nc.scalar
+            queue.dma_start(
+                out=key_scales[32 * g : 32 * g + 4, :].bitcast(I32),
+                in_=keys_scales[0, 4 * g : 4 * g + 4, :].bitcast(I32),
+            )
+        nc.sync.dma_start(out=raw_b[:], in_=query2.rearrange("(p j) q -> p j q", j=PACK))
+        nc.sync.dma_start(list1[:], offs)
+        nc.sync.dma_start(list2[:], offs2)
+        nc.sync.dma_start(out=lam_sb[:], in_=lam)
+        nc.sync.dma_start(out=level_sb[:], in_=level)
+        nc.sync.dma_start(list4[:], offs4)
+        nc.sync.dma_start(out=gain_sb[:], in_=gainm)
+        nc.sync.dma_start(out=old_sb[:], in_=old)
+        nc.vector.memset(placed[:], 0.0)
+
+        side_a = sb.tile([P, Q, PACK], BF16, name="side_a", align_bytes=64)
+        side_b = sb.tile([P, Q, PACK], BF16, name="side_b", align_bytes=64)
+        codes_a = sb.tile([P, Q], U32, name="codes_a", align_bytes=64)
+        codes_b = sb.tile([P, Q], U32, name="codes_b", align_bytes=64)
+        scales_a = sb.tile([P, Q], U8, name="scales_a", align_bytes=64)
+        scales_b = sb.tile([P, Q], U8, name="scales_b", align_bytes=64)
+        nc.vector.tensor_copy(out=side_a[:], in_=raw_a[:].rearrange("p j q -> p q j"))
+        nc.vector.quantize_mx(
+            out=codes_a[:].bitcast(FP8X4), scales=scales_a[:], in_=side_a[:].rearrange("p q j -> p (q j)")
+        )
+        nc.vector.tensor_copy(out=side_b[:], in_=raw_b[:].rearrange("p j q -> p q j"))
+        nc.vector.quantize_mx(
+            out=codes_b[:].bitcast(FP8X4), scales=scales_b[:], in_=side_b[:].rearrange("p q j -> p (q j)")
+        )
+
+        a_sb = sb.tile([P, T], F32, name="a_sb")
+        b_sb = sb.tile([P, T], F32, name="b_sb")
+        pieces = T // N_MM
+        for scores, codes, scales, tag in ((a_sb, codes_a, scales_a, "a"), (b_sb, codes_b, scales_b, "b")):
+            for c in range(pieces):
+                bank = ps.tile([P, N_MM], F32, name="bank_%s%d" % (tag, c))
+                nc.tensor.matmul_mx(
+                    out=bank[:],
+                    lhsT=codes[:].bitcast(FP8X4),
+                    lhsT_scale=scales[:],
+                    rhs=key_codes[:, 2 * c * N_MM : 2 * (c + 1) * N_MM].bitcast(FP4X4),
+                    rhs_scale=key_scales[:, c * N_MM : (c + 1) * N_MM],
+                    start=True,
+                    stop=True,
+                )
+                cols = slice(c * N_MM, (c + 1) * N_MM)
+                nc.scalar.activation(scores[:, cols], bank[:], ACT.Copy)
+
+        neg_s = sb.tile([P, SLOTS], F32, name="neg_s")
+        neg_max = [sb.tile([P, 1], F32, name="neg_max%d" % h) for h in range(2)]
+        picked = {}
+        for h in range(2):
+            lc = slice(h * LIST_COLS // 2, (h + 1) * LIST_COLS // 2)
+            for name, lst in (("a1", list1), ("a2", list2)):
+                picked[name, h] = sb.tile([P, HALF], F32, name="%s_%d" % (name, h))
+                nc.vector.tensor_copy(picked[name, h][:], a_sb[:].indirect(lst[:, lc]))
+        for h in range(2):
+            lc = slice(h * LIST_COLS // 2, (h + 1) * LIST_COLS // 2)
+            for name, lst in (("b2", list2), ("b1", list1)):
+                picked[name, h] = sb.tile([P, HALF], F32, name="%s_%d" % (name, h))
+                nc.scalar.activation(picked[name, h][:], b_sb[:].indirect(lst[:, lc]), ACT.Copy)
+        for h in range(2):
+            first = sb.tile([P, HALF], F32, name="first%d" % h)
+            second = sb.tile([P, HALF], F32, name="second%d" % h)
+            diff = sb.tile([P, HALF], F32, name="diff%d" % h)
+            nc.vector.tensor_tensor(first[:], picked["a1", h][:], picked["b2", h][:], ALU.max)
+            nc.vector.tensor_tensor(second[:], picked["a2", h][:], picked["b1", h][:], ALU.max)
+            nc.vector.tensor_tensor(diff[:], second[:], first[:], ALU.subtract)
+            nc.vector.tensor_scalar(
+                neg_s[:, h * HALF : (h + 1) * HALF],
+                diff[:],
+                lam_sb[:],
+                None if h == 0 else neg_max[0][:],
+                ALU.mult,
+                ALU.min,
+                accum_out=neg_max[h][:],
+            )
+
+        neg_level = sb.tile([P, 1], F32, name="neg_level")
+        nc.gpsimd.tensor_scalar(neg_level[:], level_sb[:], -1.0, 0.0, ALU.mult, ALU.add)
+        runs = (slice(0, FIRST), slice(FIRST, SLOTS))
+        p_sb = sb.tile([P, SLOTS], F32, name="p_sb")
+        excess = sb.tile([P, SLOTS], F32, name="excess")
+        run_sum = [sb.tile([P, 1], F32, name="run_sum%d" % r) for r in range(2)]
+        first_part = sb.tile([P, 1], F32, name="first_part")
+        row_sum = sb.tile([P, 1], F32, name="row_sum")
+        inv_sum = sb.tile([P, 1], F32, name="inv_sum")
+        for r, run in enumerate(runs):
+            nc.scalar.activation(
+                p_sb[:, run], neg_s[:, run], ACT.Exp, bias=neg_max[1][:], scale=-1.0, accum_out=run_sum[r][:]
+            )
+        nc.vector.tensor_scalar(excess[:, runs[0]], p_sb[:, runs[0]], level_sb[:], 0.0, ALU.subtract, ALU.max)
+        nc.scalar.activation(first_part[:], run_sum[0][:], ACT.Copy, scale=1.0 / 256.0)
+        nc.scalar.activation(row_sum[:], run_sum[1][:], ACT.Identity, bias=first_part[:], scale=1.0 / 256.0)
+        nc.scalar.activation(excess[:, runs[1]], p_sb[:, runs[1]], ACT.Relu, bias=neg_level[:])
+        nc.vector.reciprocal(inv_sum[:], row_sum[:])
+        for run in runs:
+            nc.vector.tensor_tensor(
+                placed[:].indirect(list4[:, run.start // 16 : run.stop // 16]), excess[:, run], gain_sb[:, run], ALU.mult
+            )
+
+        for c in range(T // N_OUT):
+            cols = slice(c * N_OUT, (c + 1) * N_OUT)
+            result = sb.tile([P, N_OUT], F32, name="result%d" % c)
+            nc.vector.scalar_tensor_tensor(result[:], placed[:, cols], inv_sum[:], old_sb[:, cols], ALU.mult, ALU.add)
+            queue = nc.sync if c % 2 == 0 else nc.scalar
+            queue.dma_start(out=out[:, cols], in_=result[:])

@@ -18,11 +18,13 @@ ACT = mybir.ActivationFunctionType
 
 P = 128
 PACK = 4
-N_MM = 256
+QUADRANT = 32
+PER_COLUMN = 16
+TOKENS_MM = 256
 HALF = SLOTS // 2
-LIST_COLS = SLOTS // 16
-N_OUT = 256
+CAST_SPLIT = 72
 FIRST = 128
+OUT_BOUNDS = (0, 128, 384, 640, 896, 1024)
 
 
 def tile_attend_exchanged_excess_moved_heads_kernel(
@@ -33,9 +35,9 @@ def tile_attend_exchanged_excess_moved_heads_kernel(
         sb = ctx.enter_context(tc.tile_pool(name="sb", bufs=1))
         ps = ctx.enter_context(tc.psum_pool(name="ps", bufs=1))
 
-        list1 = sb.tile([P, LIST_COLS], U16, name="list1")
-        list2 = sb.tile([P, LIST_COLS], U16, name="list2")
-        list4 = sb.tile([P, LIST_COLS], U16, name="list4")
+        list1 = sb.tile([P, SLOTS // PER_COLUMN], U16, name="list1")
+        list2 = sb.tile([P, SLOTS // PER_COLUMN], U16, name="list2")
+        list4 = sb.tile([P, SLOTS // PER_COLUMN], U16, name="list4")
         raw_a = sb.tile([P, PACK, Q], F32, name="raw_a")
         raw_b = sb.tile([P, PACK, Q], F32, name="raw_b")
         key_codes = sb.tile([P, 2 * T], U8, name="key_codes", align_bytes=64)
@@ -48,12 +50,12 @@ def tile_attend_exchanged_excess_moved_heads_kernel(
 
         nc.vector.memset(key_scales[:, : T // 2].bitcast(I32), 0)
         nc.gpsimd.memset(key_scales[:, T // 2 :].bitcast(I32), 0)
+
         nc.sync.dma_start(out=raw_a[:], in_=query.rearrange("(p j) q -> p j q", j=PACK))
         nc.sync.dma_start(out=key_codes[:].bitcast(I32), in_=keys_words[0].bitcast(I32))
-        for g in range(4):
-            queue = nc.sync if g % 2 == 0 else nc.scalar
-            queue.dma_start(
-                out=key_scales[32 * g : 32 * g + 4, :].bitcast(I32),
+        for g in range(P // QUADRANT):
+            nc.sync.dma_start(
+                out=key_scales[QUADRANT * g : QUADRANT * g + 4, :].bitcast(I32),
                 in_=keys_scales[0, 4 * g : 4 * g + 4, :].bitcast(I32),
             )
         nc.sync.dma_start(out=raw_b[:], in_=query2.rearrange("(p j) q -> p j q", j=PACK))
@@ -72,7 +74,8 @@ def tile_attend_exchanged_excess_moved_heads_kernel(
         codes_b = sb.tile([P, Q], U32, name="codes_b", align_bytes=64)
         scales_a = sb.tile([P, Q], U8, name="scales_a", align_bytes=64)
         scales_b = sb.tile([P, Q], U8, name="scales_b", align_bytes=64)
-        nc.vector.tensor_copy(out=side_a[:], in_=raw_a[:].rearrange("p j q -> p q j"))
+        nc.vector.tensor_copy(out=side_a[:, :CAST_SPLIT, :], in_=raw_a[:, :, :CAST_SPLIT].rearrange("p j q -> p q j"))
+        nc.scalar.activation(side_a[:, CAST_SPLIT:, :], raw_a[:, :, CAST_SPLIT:].rearrange("p j q -> p q j"), ACT.Copy)
         nc.vector.quantize_mx(
             out=codes_a[:].bitcast(FP8X4), scales=scales_a[:], in_=side_a[:].rearrange("p q j -> p (q j)")
         )
@@ -83,78 +86,77 @@ def tile_attend_exchanged_excess_moved_heads_kernel(
 
         a_sb = sb.tile([P, T], F32, name="a_sb")
         b_sb = sb.tile([P, T], F32, name="b_sb")
-        pieces = T // N_MM
-        for scores, codes, scales, tag in ((a_sb, codes_a, scales_a, "a"), (b_sb, codes_b, scales_b, "b")):
-            for c in range(pieces):
-                bank = ps.tile([P, N_MM], F32, name="bank_%s%d" % (tag, c))
+        for side, scores, codes, scales in (("a", a_sb, codes_a, scales_a), ("b", b_sb, codes_b, scales_b)):
+            for t0 in range(0, T, TOKENS_MM):
+                t1 = t0 + TOKENS_MM
+                bank = ps.tile([P, TOKENS_MM], F32, name="bank_%s%d" % (side, t0))
                 nc.tensor.matmul_mx(
                     out=bank[:],
                     lhsT=codes[:].bitcast(FP8X4),
                     lhsT_scale=scales[:],
-                    rhs=key_codes[:, 2 * c * N_MM : 2 * (c + 1) * N_MM].bitcast(FP4X4),
-                    rhs_scale=key_scales[:, c * N_MM : (c + 1) * N_MM],
+                    rhs=key_codes[:, 2 * t0 : 2 * t1].bitcast(FP4X4),
+                    rhs_scale=key_scales[:, t0:t1],
                     start=True,
                     stop=True,
                 )
-                cols = slice(c * N_MM, (c + 1) * N_MM)
-                nc.scalar.activation(scores[:, cols], bank[:], ACT.Copy)
+                nc.scalar.activation(scores[:, t0:t1], bank[:], ACT.Copy)
 
+        def entries(list_tile, slots):
+            return list_tile[:, slots.start // PER_COLUMN : slots.stop // PER_COLUMN]
+
+        halves = (slice(0, HALF), slice(HALF, SLOTS))
         neg_s = sb.tile([P, SLOTS], F32, name="neg_s")
         neg_max = [sb.tile([P, 1], F32, name="neg_max%d" % h) for h in range(2)]
-        picked = {}
-        for h in range(2):
-            lc = slice(h * LIST_COLS // 2, (h + 1) * LIST_COLS // 2)
-            for name, lst in (("a1", list1), ("a2", list2)):
-                picked[name, h] = sb.tile([P, HALF], F32, name="%s_%d" % (name, h))
-                nc.vector.tensor_copy(picked[name, h][:], a_sb[:].indirect(lst[:, lc]))
-        for h in range(2):
-            lc = slice(h * LIST_COLS // 2, (h + 1) * LIST_COLS // 2)
-            for name, lst in (("b2", list2), ("b1", list1)):
-                picked[name, h] = sb.tile([P, HALF], F32, name="%s_%d" % (name, h))
-                nc.scalar.activation(picked[name, h][:], b_sb[:].indirect(lst[:, lc]), ACT.Copy)
-        for h in range(2):
+        a_at_1 = sb.tile([P, SLOTS], F32, name="a_at_1")
+        nc.vector.tensor_copy(a_at_1[:], a_sb[:].indirect(list1[:]))
+        a_at_2 = sb.tile([P, SLOTS], F32, name="a_at_2")
+        nc.vector.tensor_copy(a_at_2[:], a_sb[:].indirect(list2[:]))
+        b_at_1, b_at_2 = [], []
+        for h, half in enumerate(halves):
+            b_at_2.append(sb.tile([P, HALF], F32, name="b_at_2_%d" % h, tag="b_at_2_%d" % h))
+            nc.scalar.activation(b_at_2[h][:], b_sb[:].indirect(entries(list2, half)), ACT.Copy)
+            b_at_1.append(sb.tile([P, HALF], F32, name="b_at_1_%d" % h, tag="b_at_1_%d" % h))
+            nc.scalar.activation(b_at_1[h][:], b_sb[:].indirect(entries(list1, half)), ACT.Copy)
+
+        for h, half in enumerate(halves):
             first = sb.tile([P, HALF], F32, name="first%d" % h)
             second = sb.tile([P, HALF], F32, name="second%d" % h)
             diff = sb.tile([P, HALF], F32, name="diff%d" % h)
-            nc.vector.tensor_tensor(first[:], picked["a1", h][:], picked["b2", h][:], ALU.max)
-            nc.vector.tensor_tensor(second[:], picked["a2", h][:], picked["b1", h][:], ALU.max)
+            nc.vector.tensor_tensor(first[:], a_at_1[:, half], b_at_2[h][:], ALU.max)
+            nc.vector.tensor_tensor(second[:], a_at_2[:, half], b_at_1[h][:], ALU.max)
             nc.vector.tensor_tensor(diff[:], second[:], first[:], ALU.subtract)
             nc.vector.tensor_scalar(
-                neg_s[:, h * HALF : (h + 1) * HALF],
+                neg_s[:, half],
                 diff[:],
                 lam_sb[:],
-                None if h == 0 else neg_max[0][:],
+                neg_max[h - 1][:] if h > 0 else None,
                 ALU.mult,
                 ALU.min,
                 accum_out=neg_max[h][:],
             )
 
-        neg_level = sb.tile([P, 1], F32, name="neg_level")
-        nc.gpsimd.tensor_scalar(neg_level[:], level_sb[:], -1.0, 0.0, ALU.mult, ALU.add)
-        runs = (slice(0, FIRST), slice(FIRST, SLOTS))
-        p_sb = sb.tile([P, SLOTS], F32, name="p_sb")
-        excess = sb.tile([P, SLOTS], F32, name="excess")
-        run_sum = [sb.tile([P, 1], F32, name="run_sum%d" % r) for r in range(2)]
-        first_part = sb.tile([P, 1], F32, name="first_part")
-        row_sum = sb.tile([P, 1], F32, name="row_sum")
-        inv_sum = sb.tile([P, 1], F32, name="inv_sum")
-        for r, run in enumerate(runs):
-            nc.scalar.activation(
-                p_sb[:, run], neg_s[:, run], ACT.Exp, bias=neg_max[1][:], scale=-1.0, accum_out=run_sum[r][:]
-            )
-        nc.vector.tensor_scalar(excess[:, runs[0]], p_sb[:, runs[0]], level_sb[:], 0.0, ALU.subtract, ALU.max)
-        nc.scalar.activation(first_part[:], run_sum[0][:], ACT.Copy, scale=1.0 / 256.0)
-        nc.scalar.activation(row_sum[:], run_sum[1][:], ACT.Identity, bias=first_part[:], scale=1.0 / 256.0)
-        nc.scalar.activation(excess[:, runs[1]], p_sb[:, runs[1]], ACT.Relu, bias=neg_level[:])
-        nc.vector.reciprocal(inv_sum[:], row_sum[:])
-        for run in runs:
-            nc.vector.tensor_tensor(
-                placed[:].indirect(list4[:, run.start // 16 : run.stop // 16]), excess[:, run], gain_sb[:, run], ALU.mult
-            )
+        neg_level = sb.tile([P, 1], F32, name="neg_level", tag="b_at_1_1")
+        nc.scalar.activation(neg_level[:], level_sb[:], ACT.Copy, scale=-1.0)
 
-        for c in range(T // N_OUT):
-            cols = slice(c * N_OUT, (c + 1) * N_OUT)
-            result = sb.tile([P, N_OUT], F32, name="result%d" % c)
-            nc.vector.scalar_tensor_tensor(result[:], placed[:, cols], inv_sum[:], old_sb[:, cols], ALU.mult, ALU.add)
+        early, late = slice(0, FIRST), slice(FIRST, SLOTS)
+        p_early = sb.tile([P, FIRST], F32, name="p_early")
+        p_all = sb.tile([P, SLOTS], F32, name="p_all")
+        excess = sb.tile([P, SLOTS], F32, name="excess")
+        row_sum = sb.tile([P, 1], F32, name="row_sum")
+        sum_by_256 = sb.tile([P, 1], F32, name="sum_by_256")
+        row_factor = sb.tile([P, 1], F32, name="row_factor")
+        nc.scalar.activation(p_early[:], neg_s[:, early], ACT.Exp, bias=neg_max[1][:], scale=-1.0)
+        nc.scalar.activation(p_all[:], neg_s[:], ACT.Exp, bias=neg_max[1][:], scale=-1.0, accum_out=row_sum[:])
+        nc.vector.tensor_scalar(excess[:, early], p_early[:], level_sb[:], 0.0, ALU.subtract, ALU.max)
+        nc.scalar.activation(excess[:, late], p_all[:, late], ACT.Relu, bias=neg_level[:])
+        nc.scalar.activation(sum_by_256[:], row_sum[:], ACT.Copy, scale=1.0 / 256.0)
+
+        nc.vector.tensor_tensor(placed[:].indirect(entries(list4, early)), excess[:, early], gain_sb[:, early], ALU.mult)
+        nc.vector.reciprocal(row_factor[:], sum_by_256[:])
+        nc.vector.tensor_tensor(placed[:].indirect(entries(list4, late)), excess[:, late], gain_sb[:, late], ALU.mult)
+
+        for c, (t0, t1) in enumerate(zip(OUT_BOUNDS, OUT_BOUNDS[1:])):
+            result = sb.tile([P, t1 - t0], F32, name="result%d" % c)
+            nc.vector.scalar_tensor_tensor(result[:], placed[:, t0:t1], row_factor[:], old_sb[:, t0:t1], ALU.mult, ALU.add)
             queue = nc.sync if c % 2 == 0 else nc.scalar
-            queue.dma_start(out=out[:, cols], in_=result[:])
+            queue.dma_start(out=out[:, t0:t1], in_=result[:])

from contextlib import ExitStack

import concourse.mybir as mybir

D, T, SLOTS, Q = 512, 1024, 512, 128
FLOPS = 2 * 2 * D * Q * T

F32 = mybir.dt.float32
BF16 = mybir.dt.bfloat16
I32 = mybir.dt.int32
U32 = mybir.dt.uint32
U16 = mybir.dt.uint16
U8 = mybir.dt.uint8
FP8X4 = mybir.dt.float8_e4m3fn_x4
FP4X4 = mybir.dt.float4_e2m1fn_x4
ALU = mybir.AluOpType
ACT = mybir.ActivationFunctionType

P = 128
PACK = 4
QUADRANT = 32
PER_COLUMN = 16
TOKENS_MM = 256
HALF = SLOTS // 2
CAST_SPLIT = 72
FIRST = 128
OUT_BOUNDS = (0, 128, 384, 640, 896, 1024)


def tile_attend_exchanged_excess_moved_heads_kernel(
    tc, query, query2, keys_words, keys_scales, lam, level, old, gainm, offs, offs2, offs4, out
):
    nc = tc.nc
    with ExitStack() as ctx:
        sb = ctx.enter_context(tc.tile_pool(name="sb", bufs=1))
        ps = ctx.enter_context(tc.psum_pool(name="ps", bufs=1))

        list1 = sb.tile([P, SLOTS // PER_COLUMN], U16, name="list1")
        list2 = sb.tile([P, SLOTS // PER_COLUMN], U16, name="list2")
        list4 = sb.tile([P, SLOTS // PER_COLUMN], U16, name="list4")
        raw_a = sb.tile([P, PACK, Q], F32, name="raw_a")
        raw_b = sb.tile([P, PACK, Q], F32, name="raw_b")
        key_codes = sb.tile([P, 2 * T], U8, name="key_codes", align_bytes=64)
        key_scales = sb.tile([P, T], U8, name="key_scales", align_bytes=64)
        lam_sb = sb.tile([P, 1], F32, name="lam_sb")
        level_sb = sb.tile([P, 1], F32, name="level_sb")
        gain_sb = sb.tile([P, SLOTS], F32, name="gain_sb")
        old_sb = sb.tile([P, T], F32, name="old_sb")
        placed = sb.tile([P, T], F32, name="placed")

        nc.vector.memset(key_scales[:, : T // 2].bitcast(I32), 0)
        nc.gpsimd.memset(key_scales[:, T // 2 :].bitcast(I32), 0)

        nc.sync.dma_start(out=raw_a[:], in_=query.rearrange("(p j) q -> p j q", j=PACK))
        nc.sync.dma_start(out=key_codes[:].bitcast(I32), in_=keys_words[0].bitcast(I32))
        for g in range(P // QUADRANT):
            nc.sync.dma_start(
                out=key_scales[QUADRANT * g : QUADRANT * g + 4, :].bitcast(I32),
                in_=keys_scales[0, 4 * g : 4 * g + 4, :].bitcast(I32),
            )
        nc.sync.dma_start(out=raw_b[:], in_=query2.rearrange("(p j) q -> p j q", j=PACK))
        nc.sync.dma_start(list1[:], offs)
        nc.sync.dma_start(list2[:], offs2)
        nc.sync.dma_start(out=lam_sb[:], in_=lam)
        nc.sync.dma_start(out=level_sb[:], in_=level)
        nc.sync.dma_start(list4[:], offs4)
        nc.sync.dma_start(out=gain_sb[:], in_=gainm)
        nc.sync.dma_start(out=old_sb[:], in_=old)
        nc.vector.memset(placed[:], 0.0)

        side_a = sb.tile([P, Q, PACK], BF16, name="side_a", align_bytes=64)
        side_b = sb.tile([P, Q, PACK], BF16, name="side_b", align_bytes=64)
        codes_a = sb.tile([P, Q], U32, name="codes_a", align_bytes=64)
        codes_b = sb.tile([P, Q], U32, name="codes_b", align_bytes=64)
        scales_a = sb.tile([P, Q], U8, name="scales_a", align_bytes=64)
        scales_b = sb.tile([P, Q], U8, name="scales_b", align_bytes=64)
        nc.vector.tensor_copy(out=side_a[:, :CAST_SPLIT, :], in_=raw_a[:, :, :CAST_SPLIT].rearrange("p j q -> p q j"))
        nc.scalar.activation(side_a[:, CAST_SPLIT:, :], raw_a[:, :, CAST_SPLIT:].rearrange("p j q -> p q j"), ACT.Copy)
        nc.vector.quantize_mx(
            out=codes_a[:].bitcast(FP8X4), scales=scales_a[:], in_=side_a[:].rearrange("p q j -> p (q j)")
        )
        nc.vector.tensor_copy(out=side_b[:], in_=raw_b[:].rearrange("p j q -> p q j"))
        nc.vector.quantize_mx(
            out=codes_b[:].bitcast(FP8X4), scales=scales_b[:], in_=side_b[:].rearrange("p q j -> p (q j)")
        )

        a_sb = sb.tile([P, T], F32, name="a_sb")
        b_sb = sb.tile([P, T], F32, name="b_sb")
        for side, scores, codes, scales in (("a", a_sb, codes_a, scales_a), ("b", b_sb, codes_b, scales_b)):
            for t0 in range(0, T, TOKENS_MM):
                t1 = t0 + TOKENS_MM
                bank = ps.tile([P, TOKENS_MM], F32, name="bank_%s%d" % (side, t0))
                nc.tensor.matmul_mx(
                    out=bank[:],
                    lhsT=codes[:].bitcast(FP8X4),
                    lhsT_scale=scales[:],
                    rhs=key_codes[:, 2 * t0 : 2 * t1].bitcast(FP4X4),
                    rhs_scale=key_scales[:, t0:t1],
                    start=True,
                    stop=True,
                )
                nc.scalar.activation(scores[:, t0:t1], bank[:], ACT.Copy)

        def entries(list_tile, slots):
            return list_tile[:, slots.start // PER_COLUMN : slots.stop // PER_COLUMN]

        halves = (slice(0, HALF), slice(HALF, SLOTS))
        neg_s = sb.tile([P, SLOTS], F32, name="neg_s")
        neg_max = [sb.tile([P, 1], F32, name="neg_max%d" % h) for h in range(2)]
        a_at_1 = sb.tile([P, SLOTS], F32, name="a_at_1")
        nc.vector.tensor_copy(a_at_1[:], a_sb[:].indirect(list1[:]))
        a_at_2 = sb.tile([P, SLOTS], F32, name="a_at_2")
        nc.vector.tensor_copy(a_at_2[:], a_sb[:].indirect(list2[:]))
        b_at_1, b_at_2 = [], []
        for h, half in enumerate(halves):
            b_at_2.append(sb.tile([P, HALF], F32, name="b_at_2_%d" % h, tag="b_at_2_%d" % h))
            nc.scalar.activation(b_at_2[h][:], b_sb[:].indirect(entries(list2, half)), ACT.Copy)
            b_at_1.append(sb.tile([P, HALF], F32, name="b_at_1_%d" % h, tag="b_at_1_%d" % h))
            nc.scalar.activation(b_at_1[h][:], b_sb[:].indirect(entries(list1, half)), ACT.Copy)

        for h, half in enumerate(halves):
            first = sb.tile([P, HALF], F32, name="first%d" % h)
            second = sb.tile([P, HALF], F32, name="second%d" % h)
            diff = sb.tile([P, HALF], F32, name="diff%d" % h)
            nc.vector.tensor_tensor(first[:], a_at_1[:, half], b_at_2[h][:], ALU.max)
            nc.vector.tensor_tensor(second[:], a_at_2[:, half], b_at_1[h][:], ALU.max)
            nc.vector.tensor_tensor(diff[:], second[:], first[:], ALU.subtract)
            nc.vector.tensor_scalar(
                neg_s[:, half],
                diff[:],
                lam_sb[:],
                neg_max[h - 1][:] if h > 0 else None,
                ALU.mult,
                ALU.min,
                accum_out=neg_max[h][:],
            )

        neg_level = sb.tile([P, 1], F32, name="neg_level", tag="b_at_1_1")
        nc.scalar.activation(neg_level[:], level_sb[:], ACT.Copy, scale=-1.0)

        early, late = slice(0, FIRST), slice(FIRST, SLOTS)
        p_early = sb.tile([P, FIRST], F32, name="p_early")
        p_all = sb.tile([P, SLOTS], F32, name="p_all")
        excess = sb.tile([P, SLOTS], F32, name="excess")
        row_sum = sb.tile([P, 1], F32, name="row_sum")
        sum_by_256 = sb.tile([P, 1], F32, name="sum_by_256")
        row_factor = sb.tile([P, 1], F32, name="row_factor")
        nc.scalar.activation(p_early[:], neg_s[:, early], ACT.Exp, bias=neg_max[1][:], scale=-1.0)
        nc.scalar.activation(p_all[:], neg_s[:], ACT.Exp, bias=neg_max[1][:], scale=-1.0, accum_out=row_sum[:])
        nc.vector.tensor_scalar(excess[:, early], p_early[:], level_sb[:], 0.0, ALU.subtract, ALU.max)
        nc.scalar.activation(excess[:, late], p_all[:, late], ACT.Relu, bias=neg_level[:])
        nc.scalar.activation(sum_by_256[:], row_sum[:], ACT.Copy, scale=1.0 / 256.0)

        nc.vector.tensor_tensor(placed[:].indirect(entries(list4, early)), excess[:, early], gain_sb[:, early], ALU.mult)
        nc.vector.reciprocal(row_factor[:], sum_by_256[:])
        nc.vector.tensor_tensor(placed[:].indirect(entries(list4, late)), excess[:, late], gain_sb[:, late], ALU.mult)

        for c, (t0, t1) in enumerate(zip(OUT_BOUNDS, OUT_BOUNDS[1:])):
            result = sb.tile([P, t1 - t0], F32, name="result%d" % c)
            nc.vector.scalar_tensor_tensor(result[:], placed[:, t0:t1], row_factor[:], old_sb[:, t0:t1], ALU.mult, ALU.add)
            queue = nc.sync if c % 2 == 0 else nc.scalar
            queue.dma_start(out=out[:, t0:t1], in_=result[:])
